import numpy as np
import ml_dtypes

BF16 = ml_dtypes.bfloat16


def bf(x):
    return np.asarray(x, np.float32).astype(BF16)


def f32(x):
    return np.asarray(x, np.float32)


def f64(x):
    return np.asarray(x).astype(np.float64)


def striped(idx):
    return np.tile(idx.reshape(-1, 16).T, (8, 1))


S, K, M, N = 512, 256, 128, 64


def setup_inputs():
    return {"base": bf(np.random.standard_normal((M, S))), "x": bf(np.random.standard_normal((K, N))), "w": bf(np.random.standard_normal((K, M)) / np.sqrt(K)), "b": f32(0.5 * np.random.standard_normal((M, 1))), "offs": striped(np.random.permutation(S)[:N])}


def reference(base, x, w, b, offs):
    idx = offs[:16].T.reshape(-1)
    z = f64(base).copy()
    z[:, idx] += f64(w).T @ f64(x)
    return np.maximum(z + f64(b), 0.0)

@@ -1,0 +1,53 @@
+import concourse.mybir as mybir
+from concourse.masks import make_identity
+
+BF16, F32, U16 = mybir.dt.bfloat16, mybir.dt.float32, mybir.dt.uint16
+ADD, MAX = mybir.AluOpType.add, mybir.AluOpType.max
+
+P = 128
+S = 512
+K = 256
+N = 64
+KB = K // P
+
+FLOPS = 2 * K * P * N
+
+
+def tile_scatter_matmul_kernel(tc, base, x, w, b, offs, out):
+    nc = tc.nc
+    with (
+        tc.tile_pool(name="held", bufs=1) as held,
+        tc.psum_pool(name="psum", bufs=1) as psum,
+    ):
+        offsets = held.tile([P, N // 16], U16, name="offsets")
+        nc.sync.dma_start(offsets[:], offs)
+
+        base_tile = held.tile([P, S], BF16, name="base_tile")
+        nc.scalar.dma_start(base_tile[:], base)
+
+        w_tile = held.tile([P, KB * P], BF16, name="w_tile")
+        nc.sync.dma_start(w_tile[:], w.rearrange("(p a) m -> p (a m)", a=KB))
+        x_tile = held.tile([P, KB * N], BF16, name="x_tile")
+        nc.sync.dma_start(x_tile[:], x.rearrange("(p a) n -> p (a n)", a=KB))
+
+        bias = held.tile([P, 1], F32, name="bias")
+        nc.scalar.dma_start(bias[:], b)
+
+        ident = held.tile([P, P], BF16, name="ident")
+        make_identity(nc, ident[:])
+
+        window = psum.tile([P, S], F32, name="window")
+        nc.tensor.matmul(window[:], ident[:], base_tile[:], start=True, stop=False)
+
+        for a in range(KB):
+            nc.tensor.matmul(
+                window[:].indirect(offsets[:]),
+                w_tile[:, a * P : (a + 1) * P],
+                x_tile[:, a * N : (a + 1) * N],
+                start=False,
+                stop=(a == KB - 1),
+            )
+
+        result = held.tile([P, S], F32, name="result")
+        nc.vector.tensor_scalar(result[:], window[:], bias[:, 0:1], 0.0, op0=ADD, op1=MAX)
+        nc.sync.dma_start(out, result[:])

@@ -19,19 +19,19 @@ def tile_scatter_matmul_kernel(tc, base, x, w, b, offs, out):
         tc.tile_pool(name="held", bufs=1) as held,
         tc.psum_pool(name="psum", bufs=1) as psum,
     ):
-        offsets = held.tile([P, N // 16], U16, name="offsets")
-        nc.sync.dma_start(offsets[:], offs)
-
         base_tile = held.tile([P, S], BF16, name="base_tile")
-        nc.scalar.dma_start(base_tile[:], base)
+        nc.sync.dma_start(base_tile[:], base)
 
         w_tile = held.tile([P, KB * P], BF16, name="w_tile")
         nc.sync.dma_start(w_tile[:], w.rearrange("(p a) m -> p (a m)", a=KB))
         x_tile = held.tile([P, KB * N], BF16, name="x_tile")
         nc.sync.dma_start(x_tile[:], x.rearrange("(p a) n -> p (a n)", a=KB))
 
+        offsets = held.tile([P, N // 16], U16, name="offsets")
+        nc.sync.dma_start(offsets[:], offs)
+
         bias = held.tile([P, 1], F32, name="bias")
-        nc.scalar.dma_start(bias[:], b)
+        nc.sync.dma_start(bias[:], b)
 
         ident = held.tile([P, P], BF16, name="ident")
         make_identity(nc, ident[:])

@@ -9,6 +9,7 @@ S = 512
 K = 256
 N = 64
 KB = K // P
+WARM = 2
 
 FLOPS = 2 * K * P * N
 
@@ -32,6 +33,18 @@ def tile_scatter_matmul_kernel(tc, base, x, w, b, offs, out):
 
         bias = held.tile([P, 1], F32, name="bias")
         nc.sync.dma_start(bias[:], b)
+
+        zeros = held.tile([P, P], BF16, name="zeros")
+        nc.vector.memset(zeros[:], 0.0)
+        spare = psum.tile([P, S], F32, name="spare")
+        for _ in range(WARM):
+            nc.tensor.matmul(
+                spare[:],
+                zeros[:],
+                zeros[:].unsqueeze(1).to_broadcast([P, S // P, P]),
+                start=True,
+                stop=True,
+            )
 
         ident = held.tile([P, P], BF16, name="ident")
         make_identity(nc, ident[:])

@@ -9,6 +9,7 @@ S = 512
 K = 256
 N = 64
 KB = K // P
+LINE = 256
 WARM = 2
 
 FLOPS = 2 * K * P * N
@@ -20,12 +21,12 @@ def tile_scatter_matmul_kernel(tc, base, x, w, b, offs, out):
         tc.tile_pool(name="held", bufs=1) as held,
         tc.psum_pool(name="psum", bufs=1) as psum,
     ):
-        base_tile = held.tile([P, S], BF16, name="base_tile")
+        base_tile = held.tile([P, S], BF16, name="base_tile", align_bytes=LINE)
         nc.sync.dma_start(base_tile[:], base)
 
-        w_tile = held.tile([P, KB * P], BF16, name="w_tile")
+        w_tile = held.tile([P, KB * P], BF16, name="w_tile", align_bytes=LINE)
         nc.sync.dma_start(w_tile[:], w.rearrange("(p a) m -> p (a m)", a=KB))
-        x_tile = held.tile([P, KB * N], BF16, name="x_tile")
+        x_tile = held.tile([P, KB * N], BF16, name="x_tile", align_bytes=LINE)
         nc.sync.dma_start(x_tile[:], x.rearrange("(p a) n -> p (a n)", a=KB))
 
         offsets = held.tile([P, N // 16], U16, name="offsets")
@@ -61,6 +62,6 @@ def tile_scatter_matmul_kernel(tc, base, x, w, b, offs, out):
                 stop=(a == KB - 1),
             )
 
-        result = held.tile([P, S], F32, name="result")
+        result = held.tile([P, S], F32, name="result", align_bytes=LINE)
         nc.vector.tensor_scalar(result[:], window[:], bias[:, 0:1], 0.0, op0=ADD, op1=MAX)
         nc.sync.dma_start(out, result[:])

@@ -10,6 +10,7 @@ K = 256
 N = 64
 KB = K // P
 LINE = 256
+NARROW = 32
 WARM = 2
 
 FLOPS = 2 * K * P * N
@@ -35,14 +36,14 @@ def tile_scatter_matmul_kernel(tc, base, x, w, b, offs, out):
         bias = held.tile([P, 1], F32, name="bias")
         nc.sync.dma_start(bias[:], b)
 
-        zeros = held.tile([P, P], BF16, name="zeros")
+        zeros = held.tile([P, NARROW], BF16, name="zeros")
         nc.vector.memset(zeros[:], 0.0)
-        spare = psum.tile([P, S], F32, name="spare")
+        spare = psum.tile([NARROW, S], F32, name="spare")
         for _ in range(WARM):
             nc.tensor.matmul(
                 spare[:],
                 zeros[:],
-                zeros[:].unsqueeze(1).to_broadcast([P, S // P, P]),
+                zeros[:].unsqueeze(1).to_broadcast([P, S // NARROW, NARROW]),
                 start=True,
                 stop=True,
             )

import concourse.mybir as mybir
from concourse.masks import make_identity

BF16, F32, U16 = mybir.dt.bfloat16, mybir.dt.float32, mybir.dt.uint16
ADD, MAX = mybir.AluOpType.add, mybir.AluOpType.max

P = 128
S = 512
K = 256
N = 64
KB = K // P
LINE = 256
NARROW = 32
WARM = 2

FLOPS = 2 * K * P * N


def tile_scatter_matmul_kernel(tc, base, x, w, b, offs, out):
    nc = tc.nc
    with (
        tc.tile_pool(name="held", bufs=1) as held,
        tc.psum_pool(name="psum", bufs=1) as psum,
    ):
        base_tile = held.tile([P, S], BF16, name="base_tile", align_bytes=LINE)
        nc.sync.dma_start(base_tile[:], base)

        w_tile = held.tile([P, KB * P], BF16, name="w_tile", align_bytes=LINE)
        nc.sync.dma_start(w_tile[:], w.rearrange("(p a) m -> p (a m)", a=KB))
        x_tile = held.tile([P, KB * N], BF16, name="x_tile", align_bytes=LINE)
        nc.sync.dma_start(x_tile[:], x.rearrange("(p a) n -> p (a n)", a=KB))

        offsets = held.tile([P, N // 16], U16, name="offsets")
        nc.sync.dma_start(offsets[:], offs)

        bias = held.tile([P, 1], F32, name="bias")
        nc.sync.dma_start(bias[:], b)

        zeros = held.tile([P, NARROW], BF16, name="zeros")
        nc.vector.memset(zeros[:], 0.0)
        spare = psum.tile([NARROW, S], F32, name="spare")
        for _ in range(WARM):
            nc.tensor.matmul(
                spare[:],
                zeros[:],
                zeros[:].unsqueeze(1).to_broadcast([P, S // NARROW, NARROW]),
                start=True,
                stop=True,
            )

        ident = held.tile([P, P], BF16, name="ident")
        make_identity(nc, ident[:])

        window = psum.tile([P, S], F32, name="window")
        nc.tensor.matmul(window[:], ident[:], base_tile[:], start=True, stop=False)

        for a in range(KB):
            nc.tensor.matmul(
                window[:].indirect(offsets[:]),
                w_tile[:, a * P : (a + 1) * P],
                x_tile[:, a * N : (a + 1) * N],
                start=False,
                stop=(a == KB - 1),
            )

        result = held.tile([P, S], F32, name="result", align_bytes=LINE)
        nc.vector.tensor_scalar(result[:], window[:], bias[:, 0:1], 0.0, op0=ADD, op1=MAX)
        nc.sync.dma_start(out, result[:])
